import numpy as np
import ml_dtypes


def mxq(x, axis, fmt="e4m3"):
    dtype, down = {"e4m3": (ml_dtypes.float8_e4m3fn, 7), "e5m2": (ml_dtypes.float8_e5m2, 14)}[fmt]
    v = np.moveaxis(np.asarray(x, np.float32).astype(ml_dtypes.bfloat16).astype(np.float64), axis, -1)
    blocks = v.reshape(v.shape[:-1] + (-1, 32))
    amax = np.abs(blocks).max(-1, keepdims=True)
    byte = np.maximum(np.where(amax > 0, np.frexp(amax)[1] - 1 + 127, 0) - down, 1)
    scale = np.exp2(byte - 127.0)
    codes = (blocks / scale).astype(np.float32).astype(dtype).astype(np.float64)
    return np.moveaxis((codes * scale).reshape(v.shape), -1, axis)


WIDE = False


def mx_kscale(k):
    if not WIDE:
        return np.ones(k)
    levels = np.array([10, -10, 5, -5, 0])
    if k % 512:
        return np.exp2(np.random.permutation(np.resize(levels, k // 32))).repeat(32)
    a = np.empty((k // 512, 16))
    for p in range(k // 512):
        a[p, :8] = np.random.permutation(np.resize(levels, 8))
        for g in range(8):
            far = levels[np.abs(levels - a[p, g]) >= 10]
            a[p, g + 8] = far[np.random.randint(len(far))]
    return np.exp2(a.ravel()).repeat(32)


def f64(x):
    return np.asarray(x).astype(np.float64)


def striped(idx):
    return np.tile(idx.reshape(-1, 16).T, (8, 1)).astype(np.uint16)


def unstriped(offs):
    return offs[:16].T.reshape(-1).astype(np.int64)


E2M1 = np.array([0.0, 0.5, 1.0, 1.5, 2.0, 3.0, 4.0, 6.0, -0.0, -0.5, -1.0, -1.5, -2.0, -3.0, -4.0, -6.0])


def pack_weight(w, fmt):
    k, n = w.shape
    w = f64(np.asarray(w, np.float32).astype(ml_dtypes.bfloat16)).reshape(k // 32, 32, n)
    amax = np.abs(w).max(1)
    if fmt == "e4m3":
        byte = np.frexp(amax)[1] - 1 + 127 - 7
    else:
        mant, ex = np.frexp(amax / 6.0)
        byte = np.where(mant > 0.5, ex, ex - 1) + 127
    byte = np.clip(np.where(amax > 0, byte, 1), 1, 254)
    scaled = (w * np.exp2(127.0 - byte)[:, None, :]).reshape(k, n).astype(np.float32)
    by_word = np.ascontiguousarray(scaled.reshape(k // 512, 128, 4, n).transpose(0, 1, 3, 2))
    if fmt == "e4m3":
        words = by_word.astype(ml_dtypes.float8_e4m3fn).view(np.uint8)
    else:
        c = by_word.astype(ml_dtypes.float4_e2m1fn).view(np.uint8) & 0xF
        words = (c[..., 0::2] | (c[..., 1::2] << 4)).reshape(k // 512, 128, 2 * n)
    return np.ascontiguousarray(words), np.ascontiguousarray(byte.astype(np.uint8).reshape(k // 512, 16, n))


def unpack_weight(words, scales, fmt):
    g, _, n = scales.shape
    words = np.ascontiguousarray(words).reshape(g, 128, n, -1)
    if fmt == "e4m3":
        vals = words.view(ml_dtypes.float8_e4m3fn).astype(np.float64)
    else:
        nib = np.empty((g, 128, n, 4), np.uint8)
        nib[..., 0::2] = words & 0xF
        nib[..., 1::2] = words >> 4
        vals = E2M1[nib]
    vals = vals * np.repeat(np.exp2(scales.astype(np.float64) - 127.0), 8, axis=1)[..., None]
    return vals.transpose(0, 1, 3, 2).reshape(g * 512, n)


def pack_table4(v):
    words, scales = pack_weight(v, "e2m1")
    g, t = words.shape[0] // 2, v.shape[1]
    words = words.reshape(g, 2, 128, t, 2).transpose(0, 2, 3, 1, 4)
    return np.concatenate([words.reshape(g, -1), scales.reshape(g, -1)], axis=1)


def unpack_table4(tab):
    g, t = tab.shape[0], tab.shape[1] // 544
    words = tab[:, :512 * t].reshape(g, 128, t, 2, 2).transpose(0, 3, 1, 2, 4).reshape(2 * g, 128, 2 * t)
    return unpack_weight(words, tab[:, 512 * t:].reshape(2 * g, 16, t), "e2m1")


def silu(v):
    return v / (1.0 + np.exp(-np.maximum(v, -700.0)))


K, M, T, S = 1024, 256, 1024, 512


def setup_inputs():
    n = np.random.standard_normal
    s = mx_kscale(K)[:, None]
    return {
        "tab": pack_table4(n((K, T)) * s),
        "w": (n((K, M)) / np.sqrt(K) / s).astype(np.float32),
        "b": (0.3 * n(256)).astype(np.float32),
        "offs": striped(np.random.permutation(T)[:S]),
    }


def reference(tab, w, b, offs):
    tab_ = unpack_table4(tab)[:, unstriped(offs)]
    w_ = mxq(f64(w), 0, "e4m3")
    y = w_.T @ tab_
    return silu(y + f64(b)[:, None])

@@ -1,0 +1,124 @@
+from contextlib import ExitStack
+
+import concourse.mybir as mybir
+
+K, M, T, S = 1024, 256, 1024, 512
+FLOPS = 2 * K * M * S
+BYTES = 4 * K * M + 4 * M + 2 * S * 8 + 544 * S + 4 * M * S
+
+F32 = mybir.dt.float32
+BF16 = mybir.dt.bfloat16
+I32 = mybir.dt.int32
+U32 = mybir.dt.uint32
+U16 = mybir.dt.uint16
+U8 = mybir.dt.uint8
+FP8X4 = mybir.dt.float8_e4m3fn_x4
+FP4X4 = mybir.dt.float4_e2m1fn_x4
+SILU = mybir.ActivationFunctionType.Silu
+
+P = 128
+PACK = 4
+PASSES = 2
+HALVES = 2
+S_HALF = S // HALVES
+N_MX = 128
+
+
+def tile_list_tab4_silu_kernel(tc, tab, w, b, offs, out):
+    nc = tc.nc
+    word_bytes = 4 * P * T
+    with ExitStack() as ctx:
+        held = ctx.enter_context(tc.tile_pool(name="held", bufs=1))
+        psum = ctx.enter_context(tc.psum_pool(name="psum", bufs=1))
+
+        offsets = held.tile([P, S // 16], U16, name="offsets")
+        planes = held.tile([P, PASSES, T], U8, name="planes", align_bytes=64)
+        words = held.tile([P, T], I32, name="words", align_bytes=64)
+        bias = held.tile([P, 2], F32, name="bias")
+        warm = held.tile([P, 1], F32, name="warm")
+        warm_out = held.tile([P, 1], F32, name="warm_out")
+        raw = [held.tile([P, PACK, M], F32, name=f"raw{a}", align_bytes=64) for a in range(PASSES)]
+        grouped = [held.tile([P, M * PACK], BF16, name=f"grouped{a}", align_bytes=64) for a in range(PASSES)]
+        w_codes = [held.tile([P, M], U32, name=f"w_codes{a}", align_bytes=64) for a in range(PASSES)]
+        w_scales = [held.tile([P, M], U8, name=f"w_scales{a}", align_bytes=64) for a in range(PASSES)]
+        v_scales = [held.tile([P, S], U8, name=f"v_scales{a}", align_bytes=64) for a in range(PASSES)]
+
+        nc.vector.memset(planes[:].bitcast(I32), 0)
+        nc.gpsimd.memset(warm[:], 0.0)
+        nc.scalar.activation(out=warm_out[:], in_=warm[:], func=SILU)
+
+        nc.sync.dma_start(offsets[:], offs)
+        scale_rows = tab[0, word_bytes : word_bytes + 32 * T].rearrange("(h q t) -> q h t", h=PASSES, q=16)
+        for quad in range(4):
+            nc.sync.dma_start(
+                out=planes[32 * quad : 32 * quad + 4, :, :].bitcast(I32),
+                in_=scale_rows[4 * quad : 4 * quad + 4, :, :].bitcast(I32),
+            )
+
+        def load_w(a):
+            nc.sync.dma_start(out=raw[a][:], in_=w[512 * a : 512 * (a + 1), :].rearrange("(p j) n -> p j n", j=PACK))
+
+        load_w(0)
+        nc.sync.dma_start(out=words[:], in_=tab[0, 0:word_bytes].rearrange("(p b) -> p b", p=P).bitcast(I32))
+        load_w(1)
+        with nc.allow_non_contiguous_dma(reason="one bias value to a partition"):
+            nc.gpsimd.dma_start(out=bias[:], in_=b.rearrange("(c p) -> p c", p=P))
+
+        for a in range(PASSES):
+            nc.vector.tensor_copy(v_scales[a][:], planes[:, a, :].indirect(offsets[:]))
+
+        def interleave(a, c):
+            cols = slice(P * c, P * (c + 1))
+            dst = grouped[a][:, PACK * P * c : PACK * P * (c + 1)]
+            nc.scalar.copy(
+                out=dst.rearrange("p (n i t) -> p n t i", i=4, t=PACK),
+                in_=raw[a][:, :, cols].rearrange("p t (n i) -> p n t i", i=4),
+            )
+
+        def quantize(a):
+            nc.vector.quantize_mx(out=w_codes[a][:].bitcast(FP8X4), scales=w_scales[a][:], in_=grouped[a][:])
+
+        picked = [None] * HALVES
+        codes = [None] * HALVES
+
+        def gather(s):
+            picked[s] = held.tile([P, S_HALF], U32, name=f"picked{s}", align_bytes=64)
+            o = S_HALF // 16
+            nc.vector.tensor_copy(picked[s][:], words[:].bitcast(U32).indirect(offsets[:, o * s : o * (s + 1)]))
+
+        def part(s):
+            codes[s] = held.tile([P, PASSES, 2 * S_HALF], U8, name=f"codes{s}", align_bytes=64)
+            nc.vector.tensor_copy(
+                codes[s][:].bitcast(U16),
+                picked[s][:].bitcast(U16).rearrange("p (n h) -> p h n", h=PASSES),
+            )
+
+        def multiply(s, c):
+            acc = psum.tile([P, S_HALF], F32, name=f"acc{s}{c}")
+            for n0 in range(0, S_HALF, N_MX):
+                for a in range(PASSES):
+                    nc.tensor.matmul_mx(
+                        out=acc[:, n0 : n0 + N_MX],
+                        lhsT=w_codes[a][:, P * c : P * (c + 1)].bitcast(FP8X4),
+                        lhsT_scale=w_scales[a][:, P * c : P * (c + 1)],
+                        rhs=codes[s][:, a, 2 * n0 : 2 * (n0 + N_MX)].bitcast(FP4X4),
+                        rhs_scale=v_scales[a][:, S_HALF * s + n0 : S_HALF * s + n0 + N_MX],
+                        start=(a == 0),
+                        stop=(a == PASSES - 1),
+                    )
+            res = held.tile([P, S_HALF], F32, name=f"res{s}{c}")
+            nc.scalar.activation(out=res[:], in_=acc[:], func=SILU, bias=bias[:, c : c + 1], scale=1.0)
+            nc.sync.dma_start(out=out[P * c : P * (c + 1), S_HALF * s : S_HALF * (s + 1)], in_=res[:])
+
+        for a in range(PASSES):
+            for c in range(2):
+                interleave(a, c)
+        gather(0)
+        quantize(0)
+        part(0)
+        gather(1)
+        quantize(1)
+        part(1)
+        for s in range(HALVES):
+            for c in range(2):
+                multiply(s, c)

@@ -19,9 +19,6 @@ SILU = mybir.ActivationFunctionType.Silu
 P = 128
 PACK = 4
 PASSES = 2
-HALVES = 2
-S_HALF = S // HALVES
-N_MX = 128
 
 
 def tile_list_tab4_silu_kernel(tc, tab, w, b, offs, out):
@@ -32,93 +29,81 @@ def tile_list_tab4_silu_kernel(tc, tab, w, b, offs, out):
         psum = ctx.enter_context(tc.psum_pool(name="psum", bufs=1))
 
         offsets = held.tile([P, S // 16], U16, name="offsets")
-        planes = held.tile([P, PASSES, T], U8, name="planes", align_bytes=64)
+        planes = held.tile([P, T], U8, name="planes", tag="early", align_bytes=64)
         words = held.tile([P, T], I32, name="words", align_bytes=64)
-        bias = held.tile([P, 2], F32, name="bias")
         warm = held.tile([P, 1], F32, name="warm")
         warm_out = held.tile([P, 1], F32, name="warm_out")
-        raw = [held.tile([P, PACK, M], F32, name=f"raw{a}", align_bytes=64) for a in range(PASSES)]
+        raw = held.tile([P, PASSES, PACK, M], F32, name="raw", align_bytes=64)
         grouped = [held.tile([P, M * PACK], BF16, name=f"grouped{a}", align_bytes=64) for a in range(PASSES)]
         w_codes = [held.tile([P, M], U32, name=f"w_codes{a}", align_bytes=64) for a in range(PASSES)]
         w_scales = [held.tile([P, M], U8, name=f"w_scales{a}", align_bytes=64) for a in range(PASSES)]
         v_scales = [held.tile([P, S], U8, name=f"v_scales{a}", align_bytes=64) for a in range(PASSES)]
+        picked = held.tile([P, S], U32, name="picked", align_bytes=64)
+        codes = held.tile([P, PASSES, 2 * S], U8, name="codes", align_bytes=64)
+        acc = [psum.tile([P, S], F32, name=f"acc{c}") for c in range(2)]
 
         nc.vector.memset(planes[:].bitcast(I32), 0)
+        nc.vector.memset(words[:, 0:1], 0)
+        nc.vector.memset(raw[:, :, 0, 0:1], 0.0)
+        nc.gpsimd.memset(v_scales[1][:].bitcast(I32), 0)
         nc.gpsimd.memset(warm[:], 0.0)
-        nc.scalar.activation(out=warm_out[:], in_=warm[:], func=SILU)
 
         nc.sync.dma_start(offsets[:], offs)
-        scale_rows = tab[0, word_bytes : word_bytes + 32 * T].rearrange("(h q t) -> q h t", h=PASSES, q=16)
-        for quad in range(4):
-            nc.sync.dma_start(
-                out=planes[32 * quad : 32 * quad + 4, :, :].bitcast(I32),
-                in_=scale_rows[4 * quad : 4 * quad + 4, :, :].bitcast(I32),
-            )
-
-        def load_w(a):
-            nc.sync.dma_start(out=raw[a][:], in_=w[512 * a : 512 * (a + 1), :].rearrange("(p j) n -> p j n", j=PACK))
-
-        load_w(0)
+        scale_rows = tab[0, word_bytes : word_bytes + 32 * T].rearrange("(h q r t) -> r q h t", h=PASSES, q=4, r=4)
+        for r in range(4):
+            nc.sync.dma_start(out=planes[r:P:16, :].bitcast(I32), in_=scale_rows[r, :, :, :].bitcast(I32))
         nc.sync.dma_start(out=words[:], in_=tab[0, 0:word_bytes].rearrange("(p b) -> p b", p=P).bitcast(I32))
-        load_w(1)
-        with nc.allow_non_contiguous_dma(reason="one bias value to a partition"):
-            nc.gpsimd.dma_start(out=bias[:], in_=b.rearrange("(c p) -> p c", p=P))
-
         for a in range(PASSES):
-            nc.vector.tensor_copy(v_scales[a][:], planes[:, a, :].indirect(offsets[:]))
+            nc.sync.dma_start(out=raw[:, a, :, :], in_=w[512 * a : 512 * (a + 1), :].rearrange("(p j) n -> p j n", j=PACK))
+        nc.scalar.activation(out=warm_out[:], in_=warm[:], func=SILU)
 
-        def interleave(a, c):
+        nc.vector.tensor_copy(v_scales[0][:], planes[:].indirect(offsets[:]))
+        for quad in range(4):
+            nc.scalar.dma_start(
+                out=v_scales[1][32 * quad : 32 * quad + 4, :].bitcast(I32),
+                in_=v_scales[0][32 * quad + 16 : 32 * quad + 20, :].bitcast(I32),
+            )
+        bias = held.tile([P, 2], F32, name="bias", tag="early", align_bytes=64)
+        with nc.allow_non_contiguous_dma(reason="one bias value to a partition"):
+            nc.sync.dma_start(out=bias[:], in_=b.rearrange("(c p) -> p c", p=P))
+        nc.vector.tensor_copy(picked[:], words[:].bitcast(U32).indirect(offsets[:]))
+
+        def interleave(copy, a, c):
             cols = slice(P * c, P * (c + 1))
             dst = grouped[a][:, PACK * P * c : PACK * P * (c + 1)]
-            nc.scalar.copy(
+            copy(
                 out=dst.rearrange("p (n i t) -> p n t i", i=4, t=PACK),
-                in_=raw[a][:, :, cols].rearrange("p t (n i) -> p n t i", i=4),
+                in_=raw[:, a, :, cols].rearrange("p t (n i) -> p n t i", i=4),
             )
 
-        def quantize(a):
-            nc.vector.quantize_mx(out=w_codes[a][:].bitcast(FP8X4), scales=w_scales[a][:], in_=grouped[a][:])
-
-        picked = [None] * HALVES
-        codes = [None] * HALVES
-
-        def gather(s):
-            picked[s] = held.tile([P, S_HALF], U32, name=f"picked{s}", align_bytes=64)
-            o = S_HALF // 16
-            nc.vector.tensor_copy(picked[s][:], words[:].bitcast(U32).indirect(offsets[:, o * s : o * (s + 1)]))
-
-        def part(s):
-            codes[s] = held.tile([P, PASSES, 2 * S_HALF], U8, name=f"codes{s}", align_bytes=64)
-            nc.vector.tensor_copy(
-                codes[s][:].bitcast(U16),
-                picked[s][:].bitcast(U16).rearrange("p (n h) -> p h n", h=PASSES),
+        interleave(nc.scalar.copy, 0, 0)
+        interleave(nc.scalar.copy, 0, 1)
+        interleave(nc.scalar.copy, 1, 0)
+        nc.vector.tensor_copy(codes[:].bitcast(U16), picked[:].bitcast(U16).rearrange("p (n h) -> p h n", h=PASSES))
+        nc.vector.quantize_mx(out=w_codes[0][:].bitcast(FP8X4), scales=w_scales[0][:], in_=grouped[0][:])
+        interleave(nc.vector.tensor_copy, 1, 1)
+        for c in range(2):
+            cols = slice(P * c, P * (c + 1))
+            nc.vector.quantize_mx(
+                out=w_codes[1][:, cols].bitcast(FP8X4),
+                scales=w_scales[1][:, cols],
+                in_=grouped[1][:, PACK * P * c : PACK * P * (c + 1)],
             )
-
-        def multiply(s, c):
-            acc = psum.tile([P, S_HALF], F32, name=f"acc{s}{c}")
-            for n0 in range(0, S_HALF, N_MX):
-                for a in range(PASSES):
-                    nc.tensor.matmul_mx(
-                        out=acc[:, n0 : n0 + N_MX],
-                        lhsT=w_codes[a][:, P * c : P * (c + 1)].bitcast(FP8X4),
-                        lhsT_scale=w_scales[a][:, P * c : P * (c + 1)],
-                        rhs=codes[s][:, a, 2 * n0 : 2 * (n0 + N_MX)].bitcast(FP4X4),
-                        rhs_scale=v_scales[a][:, S_HALF * s + n0 : S_HALF * s + n0 + N_MX],
-                        start=(a == 0),
-                        stop=(a == PASSES - 1),
-                    )
-            res = held.tile([P, S_HALF], F32, name=f"res{s}{c}")
-            nc.scalar.activation(out=res[:], in_=acc[:], func=SILU, bias=bias[:, c : c + 1], scale=1.0)
-            nc.sync.dma_start(out=out[P * c : P * (c + 1), S_HALF * s : S_HALF * (s + 1)], in_=res[:])
 
         for a in range(PASSES):
             for c in range(2):
-                interleave(a, c)
-        gather(0)
-        quantize(0)
-        part(0)
-        gather(1)
-        quantize(1)
-        part(1)
-        for s in range(HALVES):
-            for c in range(2):
-                multiply(s, c)
+                nc.tensor.matmul_mx(
+                    out=acc[c][:],
+                    lhsT=w_codes[a][:, P * c : P * (c + 1)].bitcast(FP8X4),
+                    lhsT_scale=w_scales[a][:, P * c : P * (c + 1)],
+                    rhs=codes[:, a, :].bitcast(FP4X4),
+                    rhs_scale=v_scales[a][:],
+                    start=(a == 0),
+                    stop=(a == PASSES - 1),
+                )
+        for c in range(2):
+            for n0 in range(0, S, S // 2):
+                cols = slice(n0, n0 + S // 2)
+                res = held.tile([P, S // 2], F32, name=f"res{c}_{n0}")
+                nc.scalar.activation(out=res[:], in_=acc[c][:, cols], func=SILU, bias=bias[:, c : c + 1], scale=1.0)
+                nc.sync.dma_start(out=out[P * c : P * (c + 1), cols], in_=res[:])

@@ -29,7 +29,7 @@ def tile_list_tab4_silu_kernel(tc, tab, w, b, offs, out):
         psum = ctx.enter_context(tc.psum_pool(name="psum", bufs=1))
 
         offsets = held.tile([P, S // 16], U16, name="offsets")
-        planes = held.tile([P, T], U8, name="planes", tag="early", align_bytes=64)
+        planes = held.tile([P, T], U8, name="planes", align_bytes=64)
         words = held.tile([P, T], I32, name="words", align_bytes=64)
         warm = held.tile([P, 1], F32, name="warm")
         warm_out = held.tile([P, 1], F32, name="warm_out")
@@ -42,16 +42,14 @@ def tile_list_tab4_silu_kernel(tc, tab, w, b, offs, out):
         codes = held.tile([P, PASSES, 2 * S], U8, name="codes", align_bytes=64)
         acc = [psum.tile([P, S], F32, name=f"acc{c}") for c in range(2)]
 
-        nc.vector.memset(planes[:].bitcast(I32), 0)
-        nc.vector.memset(words[:, 0:1], 0)
-        nc.vector.memset(raw[:, :, 0, 0:1], 0.0)
-        nc.gpsimd.memset(v_scales[1][:].bitcast(I32), 0)
+        nc.vector.memset(v_scales[1][:].bitcast(I32), 0)
         nc.gpsimd.memset(warm[:], 0.0)
 
         nc.sync.dma_start(offsets[:], offs)
-        scale_rows = tab[0, word_bytes : word_bytes + 32 * T].rearrange("(h q r t) -> r q h t", h=PASSES, q=4, r=4)
-        for r in range(4):
-            nc.sync.dma_start(out=planes[r:P:16, :].bitcast(I32), in_=scale_rows[r, :, :, :].bitcast(I32))
+        rows = tab[0, word_bytes - 12 * T : word_bytes + 32 * T].rearrange("(s t) -> s t", t=T).bitcast(I32)
+        flat = planes[:].bitcast(I32)
+        for p0, p1, s0 in ((0, 16, 12), (16, 48, 0), (48, 80, 4), (80, 112, 8), (112, 128, 28)):
+            nc.sync.dma_start(out=flat[p0:p1, :], in_=rows[s0 : s0 + p1 - p0, :])
         nc.sync.dma_start(out=words[:], in_=tab[0, 0:word_bytes].rearrange("(p b) -> p b", p=P).bitcast(I32))
         for a in range(PASSES):
             nc.sync.dma_start(out=raw[:, a, :, :], in_=w[512 * a : 512 * (a + 1), :].rearrange("(p j) n -> p j n", j=PACK))
@@ -61,9 +59,9 @@ def tile_list_tab4_silu_kernel(tc, tab, w, b, offs, out):
         for quad in range(4):
             nc.scalar.dma_start(
                 out=v_scales[1][32 * quad : 32 * quad + 4, :].bitcast(I32),
-                in_=v_scales[0][32 * quad + 16 : 32 * quad + 20, :].bitcast(I32),
+                in_=v_scales[0][112 + 4 * quad : 116 + 4 * quad, :].bitcast(I32),
             )
-        bias = held.tile([P, 2], F32, name="bias", tag="early", align_bytes=64)
+        bias = held.tile([P, 2], F32, name="bias")
         with nc.allow_non_contiguous_dma(reason="one bias value to a partition"):
             nc.sync.dma_start(out=bias[:], in_=b.rearrange("(c p) -> p c", p=P))
         nc.vector.tensor_copy(picked[:], words[:].bitcast(U32).indirect(offsets[:]))

@@ -19,6 +19,9 @@ SILU = mybir.ActivationFunctionType.Silu
 P = 128
 PACK = 4
 PASSES = 2
+HALVES = 2
+S_HALF = S // HALVES
+N_MX = 128
 
 
 def tile_list_tab4_silu_kernel(tc, tab, w, b, offs, out):
@@ -38,9 +41,8 @@ def tile_list_tab4_silu_kernel(tc, tab, w, b, offs, out):
         w_codes = [held.tile([P, M], U32, name=f"w_codes{a}", align_bytes=64) for a in range(PASSES)]
         w_scales = [held.tile([P, M], U8, name=f"w_scales{a}", align_bytes=64) for a in range(PASSES)]
         v_scales = [held.tile([P, S], U8, name=f"v_scales{a}", align_bytes=64) for a in range(PASSES)]
-        picked = held.tile([P, S], U32, name="picked", align_bytes=64)
-        codes = held.tile([P, PASSES, 2 * S], U8, name="codes", align_bytes=64)
-        acc = [psum.tile([P, S], F32, name=f"acc{c}") for c in range(2)]
+        picked = [held.tile([P, S_HALF], U32, name=f"picked{s}", align_bytes=64) for s in range(HALVES)]
+        codes = [held.tile([P, PASSES, 2 * S_HALF], U8, name=f"codes{s}", align_bytes=64) for s in range(HALVES)]
 
         nc.vector.memset(v_scales[1][:].bitcast(I32), 0)
         nc.gpsimd.memset(warm[:], 0.0)
@@ -64,44 +66,71 @@ def tile_list_tab4_silu_kernel(tc, tab, w, b, offs, out):
         bias = held.tile([P, 2], F32, name="bias")
         with nc.allow_non_contiguous_dma(reason="one bias value to a partition"):
             nc.sync.dma_start(out=bias[:], in_=b.rearrange("(c p) -> p c", p=P))
-        nc.vector.tensor_copy(picked[:], words[:].bitcast(U32).indirect(offsets[:]))
+        for s in range(HALVES):
+            entries = offsets[:, S_HALF // 16 * s : S_HALF // 16 * (s + 1)]
+            nc.vector.tensor_copy(picked[s][:], words[:].bitcast(U32).indirect(entries))
 
-        def interleave(copy, a, c):
-            cols = slice(P * c, P * (c + 1))
-            dst = grouped[a][:, PACK * P * c : PACK * P * (c + 1)]
-            copy(
+        def interleave(a, n0, n1):
+            cols = slice(n0, n1)
+            dst = grouped[a][:, PACK * n0 : PACK * n1]
+            nc.scalar.copy(
                 out=dst.rearrange("p (n i t) -> p n t i", i=4, t=PACK),
                 in_=raw[:, a, :, cols].rearrange("p t (n i) -> p n t i", i=4),
             )
 
-        interleave(nc.scalar.copy, 0, 0)
-        interleave(nc.scalar.copy, 0, 1)
-        interleave(nc.scalar.copy, 1, 0)
-        nc.vector.tensor_copy(codes[:].bitcast(U16), picked[:].bitcast(U16).rearrange("p (n h) -> p h n", h=PASSES))
-        nc.vector.quantize_mx(out=w_codes[0][:].bitcast(FP8X4), scales=w_scales[0][:], in_=grouped[0][:])
-        interleave(nc.vector.tensor_copy, 1, 1)
-        for c in range(2):
-            cols = slice(P * c, P * (c + 1))
-            nc.vector.quantize_mx(
-                out=w_codes[1][:, cols].bitcast(FP8X4),
-                scales=w_scales[1][:, cols],
-                in_=grouped[1][:, PACK * P * c : PACK * P * (c + 1)],
+        for a in range(PASSES):
+            for n0 in range(0, M, P):
+                interleave(a, n0, n0 + P)
+
+        def part(s):
+            nc.vector.tensor_copy(
+                codes[s][:].bitcast(U16),
+                picked[s][:].bitcast(U16).rearrange("p (n h) -> p h n", h=PASSES),
             )
 
+        def quantize(a, n0, n1):
+            nc.vector.quantize_mx(
+                out=w_codes[a][:, n0:n1].bitcast(FP8X4),
+                scales=w_scales[a][:, n0:n1],
+                in_=grouped[a][:, PACK * n0 : PACK * n1],
+            )
+
+        def multiply(acc, c, s0, a):
+            s, n0 = divmod(s0, S_HALF)
+            nc.tensor.matmul_mx(
+                out=acc,
+                lhsT=w_codes[a][:, P * c : P * (c + 1)].bitcast(FP8X4),
+                lhsT_scale=w_scales[a][:, P * c : P * (c + 1)],
+                rhs=codes[s][:, a, 2 * n0 : 2 * (n0 + N_MX)].bitcast(FP4X4),
+                rhs_scale=v_scales[a][:, s0 : s0 + N_MX],
+                start=(a == 0),
+                stop=(a == PASSES - 1),
+            )
+
+        def finish(acc, res, c):
+            nc.scalar.activation(out=res, in_=acc, func=SILU, bias=bias[:, c : c + 1], scale=1.0)
+
+        part(0)
+        quantize(0, 0, P)
+        part(1)
+        quantize(0, P, M)
+        quantize(1, 0, P)
+        quantize(1, P, M)
+
+        first = [psum.tile([P, N_MX], F32, name=f"first{i}") for i in range(S // N_MX)]
         for a in range(PASSES):
-            for c in range(2):
-                nc.tensor.matmul_mx(
-                    out=acc[c][:],
-                    lhsT=w_codes[a][:, P * c : P * (c + 1)].bitcast(FP8X4),
-                    lhsT_scale=w_scales[a][:, P * c : P * (c + 1)],
-                    rhs=codes[:, a, :].bitcast(FP4X4),
-                    rhs_scale=v_scales[a][:],
-                    start=(a == 0),
-                    stop=(a == PASSES - 1),
-                )
-        for c in range(2):
-            for n0 in range(0, S, S // 2):
-                cols = slice(n0, n0 + S // 2)
-                res = held.tile([P, S // 2], F32, name=f"res{c}_{n0}")
-                nc.scalar.activation(out=res[:], in_=acc[c][:, cols], func=SILU, bias=bias[:, c : c + 1], scale=1.0)
-                nc.sync.dma_start(out=out[P * c : P * (c + 1), cols], in_=res[:])
+            for i in range(S // N_MX):
+                multiply(first[i][:], 0, N_MX * i, a)
+        for s in range(HALVES):
+            res = held.tile([P, S_HALF], F32, name=f"res0{s}")
+            for i in range(2):
+                finish(first[2 * s + i][:], res[:, N_MX * i : N_MX * (i + 1)], 0)
+            nc.sync.dma_start(out=out[0:P, S_HALF * s : S_HALF * (s + 1)], in_=res[:])
+        for s in range(HALVES):
+            acc = psum.tile([P, S_HALF], F32, name=f"second{s}")
+            for i in range(2):
+                for a in range(PASSES):
+                    multiply(acc[:, N_MX * i : N_MX * (i + 1)], 1, S_HALF * s + N_MX * i, a)
+            res = held.tile([P, S_HALF], F32, name=f"res1{s}")
+            finish(acc[:], res[:], 1)
+            nc.sync.dma_start(out=out[P:M, S_HALF * s : S_HALF * (s + 1)], in_=res[:])

from contextlib import ExitStack

import concourse.mybir as mybir

K, M, T, S = 1024, 256, 1024, 512
FLOPS = 2 * K * M * S
BYTES = 4 * K * M + 4 * M + 2 * S * 8 + 544 * S + 4 * M * S

F32 = mybir.dt.float32
BF16 = mybir.dt.bfloat16
I32 = mybir.dt.int32
U32 = mybir.dt.uint32
U16 = mybir.dt.uint16
U8 = mybir.dt.uint8
FP8X4 = mybir.dt.float8_e4m3fn_x4
FP4X4 = mybir.dt.float4_e2m1fn_x4
SILU = mybir.ActivationFunctionType.Silu

P = 128
PACK = 4
PASSES = 2
HALVES = 2
S_HALF = S // HALVES
N_MX = 128


def tile_list_tab4_silu_kernel(tc, tab, w, b, offs, out):
    nc = tc.nc
    word_bytes = 4 * P * T
    with ExitStack() as ctx:
        held = ctx.enter_context(tc.tile_pool(name="held", bufs=1))
        psum = ctx.enter_context(tc.psum_pool(name="psum", bufs=1))

        offsets = held.tile([P, S // 16], U16, name="offsets")
        planes = held.tile([P, T], U8, name="planes", align_bytes=64)
        words = held.tile([P, T], I32, name="words", align_bytes=64)
        warm = held.tile([P, 1], F32, name="warm")
        warm_out = held.tile([P, 1], F32, name="warm_out")
        raw = held.tile([P, PASSES, PACK, M], F32, name="raw", align_bytes=64)
        grouped = [held.tile([P, M * PACK], BF16, name=f"grouped{a}", align_bytes=64) for a in range(PASSES)]
        w_codes = [held.tile([P, M], U32, name=f"w_codes{a}", align_bytes=64) for a in range(PASSES)]
        w_scales = [held.tile([P, M], U8, name=f"w_scales{a}", align_bytes=64) for a in range(PASSES)]
        v_scales = [held.tile([P, S], U8, name=f"v_scales{a}", align_bytes=64) for a in range(PASSES)]
        picked = [held.tile([P, S_HALF], U32, name=f"picked{s}", align_bytes=64) for s in range(HALVES)]
        codes = [held.tile([P, PASSES, 2 * S_HALF], U8, name=f"codes{s}", align_bytes=64) for s in range(HALVES)]

        nc.vector.memset(v_scales[1][:].bitcast(I32), 0)
        nc.gpsimd.memset(warm[:], 0.0)

        nc.sync.dma_start(offsets[:], offs)
        rows = tab[0, word_bytes - 12 * T : word_bytes + 32 * T].rearrange("(s t) -> s t", t=T).bitcast(I32)
        flat = planes[:].bitcast(I32)
        for p0, p1, s0 in ((0, 16, 12), (16, 48, 0), (48, 80, 4), (80, 112, 8), (112, 128, 28)):
            nc.sync.dma_start(out=flat[p0:p1, :], in_=rows[s0 : s0 + p1 - p0, :])
        nc.sync.dma_start(out=words[:], in_=tab[0, 0:word_bytes].rearrange("(p b) -> p b", p=P).bitcast(I32))
        for a in range(PASSES):
            nc.sync.dma_start(out=raw[:, a, :, :], in_=w[512 * a : 512 * (a + 1), :].rearrange("(p j) n -> p j n", j=PACK))
        nc.scalar.activation(out=warm_out[:], in_=warm[:], func=SILU)

        nc.vector.tensor_copy(v_scales[0][:], planes[:].indirect(offsets[:]))
        for quad in range(4):
            nc.scalar.dma_start(
                out=v_scales[1][32 * quad : 32 * quad + 4, :].bitcast(I32),
                in_=v_scales[0][112 + 4 * quad : 116 + 4 * quad, :].bitcast(I32),
            )
        bias = held.tile([P, 2], F32, name="bias")
        with nc.allow_non_contiguous_dma(reason="one bias value to a partition"):
            nc.sync.dma_start(out=bias[:], in_=b.rearrange("(c p) -> p c", p=P))
        for s in range(HALVES):
            entries = offsets[:, S_HALF // 16 * s : S_HALF // 16 * (s + 1)]
            nc.vector.tensor_copy(picked[s][:], words[:].bitcast(U32).indirect(entries))

        def interleave(a, n0, n1):
            cols = slice(n0, n1)
            dst = grouped[a][:, PACK * n0 : PACK * n1]
            nc.scalar.copy(
                out=dst.rearrange("p (n i t) -> p n t i", i=4, t=PACK),
                in_=raw[:, a, :, cols].rearrange("p t (n i) -> p n t i", i=4),
            )

        for a in range(PASSES):
            for n0 in range(0, M, P):
                interleave(a, n0, n0 + P)

        def part(s):
            nc.vector.tensor_copy(
                codes[s][:].bitcast(U16),
                picked[s][:].bitcast(U16).rearrange("p (n h) -> p h n", h=PASSES),
            )

        def quantize(a, n0, n1):
            nc.vector.quantize_mx(
                out=w_codes[a][:, n0:n1].bitcast(FP8X4),
                scales=w_scales[a][:, n0:n1],
                in_=grouped[a][:, PACK * n0 : PACK * n1],
            )

        def multiply(acc, c, s0, a):
            s, n0 = divmod(s0, S_HALF)
            nc.tensor.matmul_mx(
                out=acc,
                lhsT=w_codes[a][:, P * c : P * (c + 1)].bitcast(FP8X4),
                lhsT_scale=w_scales[a][:, P * c : P * (c + 1)],
                rhs=codes[s][:, a, 2 * n0 : 2 * (n0 + N_MX)].bitcast(FP4X4),
                rhs_scale=v_scales[a][:, s0 : s0 + N_MX],
                start=(a == 0),
                stop=(a == PASSES - 1),
            )

        def finish(acc, res, c):
            nc.scalar.activation(out=res, in_=acc, func=SILU, bias=bias[:, c : c + 1], scale=1.0)

        part(0)
        quantize(0, 0, P)
        part(1)
        quantize(0, P, M)
        quantize(1, 0, P)
        quantize(1, P, M)

        first = [psum.tile([P, N_MX], F32, name=f"first{i}") for i in range(S // N_MX)]
        for a in range(PASSES):
            for i in range(S // N_MX):
                multiply(first[i][:], 0, N_MX * i, a)
        for s in range(HALVES):
            res = held.tile([P, S_HALF], F32, name=f"res0{s}")
            for i in range(2):
                finish(first[2 * s + i][:], res[:, N_MX * i : N_MX * (i + 1)], 0)
            nc.sync.dma_start(out=out[0:P, S_HALF * s : S_HALF * (s + 1)], in_=res[:])
        for s in range(HALVES):
            acc = psum.tile([P, S_HALF], F32, name=f"second{s}")
            for i in range(2):
                for a in range(PASSES):
                    multiply(acc[:, N_MX * i : N_MX * (i + 1)], 1, S_HALF * s + N_MX * i, a)
            res = held.tile([P, S_HALF], F32, name=f"res1{s}")
            finish(acc[:], res[:], 1)
            nc.sync.dma_start(out=out[P:M, S_HALF * s : S_HALF * (s + 1)], in_=res[:])
